import numpy as np
import ml_dtypes


def mxq(x, axis, fmt="e4m3"):
    dtype, down = {"e4m3": (ml_dtypes.float8_e4m3fn, 7), "e5m2": (ml_dtypes.float8_e5m2, 14)}[fmt]
    v = np.moveaxis(np.asarray(x, np.float32).astype(ml_dtypes.bfloat16).astype(np.float64), axis, -1)
    blocks = v.reshape(v.shape[:-1] + (-1, 32))
    amax = np.abs(blocks).max(-1, keepdims=True)
    byte = np.maximum(np.where(amax > 0, np.frexp(amax)[1] - 1 + 127, 0) - down, 1)
    scale = np.exp2(byte - 127.0)
    codes = (blocks / scale).astype(np.float32).astype(dtype).astype(np.float64)
    return np.moveaxis((codes * scale).reshape(v.shape), -1, axis)


WIDE = False


def mx_kscale(k):
    if not WIDE:
        return np.ones(k)
    levels = np.array([10, -10, 5, -5, 0])
    if k % 512:
        return np.exp2(np.random.permutation(np.resize(levels, k // 32))).repeat(32)
    a = np.empty((k // 512, 16))
    for p in range(k // 512):
        a[p, :8] = np.random.permutation(np.resize(levels, 8))
        for g in range(8):
            far = levels[np.abs(levels - a[p, g]) >= 10]
            a[p, g + 8] = far[np.random.randint(len(far))]
    return np.exp2(a.ravel()).repeat(32)


def f64(x):
    return np.asarray(x).astype(np.float64)


def striped(idx):
    return np.tile(idx.reshape(-1, 16).T, (8, 1)).astype(np.uint16)


def unstriped(offs):
    return offs[:16].T.reshape(-1).astype(np.int64)


def pack_weight(w):
    k, n = w.shape
    w = f64(np.asarray(w, np.float32).astype(ml_dtypes.bfloat16)).reshape(k // 32, 32, n)
    amax = np.abs(w).max(1)
    byte = np.clip(np.where(amax > 0, np.frexp(amax)[1] - 1 + 127 - 7, 1), 1, 254)
    scaled = (w * np.exp2(127.0 - byte)[:, None, :]).reshape(k, n).astype(np.float32)
    words = np.ascontiguousarray(scaled.reshape(k // 512, 128, 4, n).transpose(0, 1, 3, 2)).astype(ml_dtypes.float8_e4m3fn).view(np.uint8)
    return words, np.ascontiguousarray(byte.astype(np.uint8).reshape(k // 512, 16, n))


def unpack_weight(words, scales):
    g, p, n, _ = words.shape
    vals = np.ascontiguousarray(words).view(ml_dtypes.float8_e4m3fn).astype(np.float64) * np.repeat(np.exp2(scales.astype(np.float64) - 127.0), 8, axis=1)[..., None]
    return vals.transpose(0, 1, 3, 2).reshape(g * 512, n)


K, T, S, V, H, N = 1024, 2048, 768, 256, 512, 256


def setup_inputs():
    n = np.random.standard_normal
    s = mx_kscale(K)[:, None]
    u = mx_kscale(H)
    packed_xT = pack_weight(n((K, T)) * s)
    return {
        "x_words": packed_xT[0],
        "x_scales": packed_xT[1],
        "w1": (n((K, H)) / np.sqrt(K) / s * u).astype(np.float32),
        "w2": (n((H, N)) / np.sqrt(2 * H) / u[:, None]).astype(np.float32),
        "w3": (n((H, N)) / np.sqrt(2 * H) / u[:, None]).astype(np.float32),
        "offs": striped(np.random.permutation(T)[:S]),
    }


def reference(x_words, x_scales, w1, w2, w3, offs):
    xq = unpack_weight(x_words, x_scales)[:, unstriped(offs)]
    h = mxq(f64(w1), 0, "e4m3").T @ xq
    mean = (h[:, :V] + h[:, V:2 * V] + h[:, 2 * V:3 * V]) / 3
    dev = np.sqrt(((h[:, :V] - mean) ** 2 + (h[:, V:2 * V] - mean) ** 2 + (h[:, 2 * V:3 * V] - mean) ** 2) / 3)
    return mxq(f64(w2), 0, "e4m3").T @ mxq(mean, 0, "e4m3") + mxq(f64(w3), 0, "e4m3").T @ mxq(dev, 0, "e4m3")

@@ -1,0 +1,205 @@
+import math
+from contextlib import ExitStack
+
+import concourse.mybir as mybir
+from concourse.masks import make_identity
+
+K, T, S, V, H, N = 1024, 2048, 768, 256, 512, 256
+FLOPS = 2 * K * H * S + 2 * 2 * H * N * V
+
+F32 = mybir.dt.float32
+BF16 = mybir.dt.bfloat16
+I32 = mybir.dt.int32
+U32 = mybir.dt.uint32
+U16 = mybir.dt.uint16
+U8 = mybir.dt.uint8
+FP8X4 = mybir.dt.float8_e4m3fn_x4
+ALU = mybir.AluOpType
+ACT = mybir.ActivationFunctionType
+
+P = 128
+PACK = 4
+PASSES = K // (P * PACK)
+HALVES = V // P
+PIECES = S // V
+W1_VECTOR_COLS = 344
+
+
+def weave_views(grouped, raw):
+    dst = grouped.rearrange("p (c i j) -> p c j i", i=PACK, j=PACK)
+    src = raw.rearrange("p j (c i) -> p c j i", i=PACK)
+    return dst, src
+
+
+def tile_picked_statpool_none_p_kernel(tc, x_words, x_scales, w1, w2, w3, offs, out):
+    nc = tc.nc
+    with ExitStack() as ctx:
+        sb = ctx.enter_context(tc.tile_pool(name="sb", bufs=1))
+        ps = ctx.enter_context(tc.psum_pool(name="ps", bufs=1))
+
+        offsets = sb.tile([P, S // 16], U16, name="offsets")
+        nc.sync.dma_start(offsets[:], offs)
+
+        x_table = [sb.tile([P, T], U32, name="x_table%d" % g, tag="x_table%d" % g, align_bytes=64) for g in range(PASSES)]
+        w1_raw = [sb.tile([P, PACK, H], F32, name="w1_raw%d" % g, tag="raw%d" % g) for g in range(PASSES)]
+
+        def load_x(g):
+            nc.sync.dma_start(x_table[g][:].bitcast(I32), x_words[g].rearrange("p n t -> p (n t)").bitcast(I32))
+
+        def load_rows(raw, rows):
+            nc.sync.dma_start(raw[:], rows.rearrange("(p j) c -> p j c", j=PACK))
+
+        scale_table = sb.tile([P, T], U8, name="scale_table", tag="stage", align_bytes=64)
+        nc.vector.memset(scale_table[:].bitcast(I32), 0)
+        zero_in = sb.tile([P, 1], F32, name="zero_in")
+        nc.vector.memset(zero_in[:], 0.0)
+        for q in range(4):
+            nc.gpsimd.dma_start(
+                scale_table[32 * q : 32 * q + 4 * PASSES, :].bitcast(I32),
+                x_scales[:, 4 * q : 4 * q + 4, :].bitcast(I32),
+            )
+        zero = sb.tile([P, 1], F32, name="zero")
+        nc.scalar.activation(zero[:], zero_in[:], ACT.Sqrt)
+
+        load_x(0)
+        load_rows(w1_raw[0], w1[0:512, :])
+        load_rows(w1_raw[1], w1[512:1024, :])
+        load_x(1)
+
+        ident = sb.tile([P, P], F32, name="ident")
+        make_identity(nc, ident[:])
+
+        banks = [ps.tile([P, 512], F32, name="bank%d" % b) for b in range(8)]
+
+        x_scale = sb.tile([P, S], U8, name="x_scale", align_bytes=64)
+        nc.vector.tensor_copy(x_scale[:], scale_table[:].indirect(offsets[:]))
+        x_code0 = sb.tile([P, S], U32, name="x_code0", align_bytes=64)
+        nc.vector.tensor_copy(x_code0[:], x_table[0][:].indirect(offsets[:]))
+
+        w1_code, w1_scale = [], []
+        for g in range(PASSES):
+            grouped = sb.tile([P, H * PACK], BF16, name="w1_grouped%d" % g, tag="stage", align_bytes=64)
+            for lo, hi, on_vector in ((0, W1_VECTOR_COLS, True), (W1_VECTOR_COLS, H, False)):
+                dst, src = weave_views(grouped[:, PACK * lo : PACK * hi], w1_raw[g][:, :, lo:hi])
+                if on_vector:
+                    nc.vector.tensor_copy(dst, src)
+                else:
+                    nc.scalar.copy(dst, src)
+            code = sb.tile([P, H], U32, name="w1_code%d" % g, align_bytes=64)
+            scale = sb.tile([P, H], U8, name="w1_scale%d" % g, align_bytes=64)
+            nc.vector.quantize_mx(code[:].bitcast(FP8X4), scale[:], grouped[:])
+            w1_code.append(code)
+            w1_scale.append(scale)
+
+        w23_raw = [sb.tile([P, PACK, N], F32, name="w23_raw%d" % u, tag="raw%d" % u) for u in range(2)]
+        load_rows(w23_raw[0], w2)
+        load_rows(w23_raw[1], w3)
+
+        order = (2, 1, 0)
+
+        def h_bank(d, h):
+            return banks[2 * d + h]
+
+        def first_product(g, d, h, codes):
+            lo = V * d + P * h
+            nc.tensor.matmul_mx(
+                h_bank(d, h)[:],
+                lhsT=codes.bitcast(FP8X4),
+                lhsT_scale=x_scale[4 * g : P, lo : lo + P],
+                rhs=w1_code[g][:].bitcast(FP8X4),
+                rhs_scale=w1_scale[g][:],
+                start=(g == 0),
+                stop=(g == PASSES - 1),
+            )
+
+        for d in order:
+            for h in range(HALVES):
+                first_product(0, d, h, x_code0[:, V * d + P * h : V * d + P * (h + 1)])
+        x_code1 = sb.tile([P, S], U32, name="x_code1", tag="stage", align_bytes=64)
+        for d in order:
+            piece = x_code1[:, V * d : V * (d + 1)]
+            nc.vector.tensor_copy(piece, x_table[1][:].indirect(offsets[:, 16 * d : 16 * (d + 1)]))
+            for h in range(HALVES):
+                first_product(1, d, h, piece[:, P * h : P * (h + 1)])
+
+        w23_grouped = sb.tile([P, 2 * N * PACK], BF16, name="w23_grouped", tag="x_table1", align_bytes=64)
+        for u in range(2):
+            dst, src = weave_views(w23_grouped[:, u * N * PACK : (u + 1) * N * PACK], w23_raw[u][:])
+            nc.gpsimd.tensor_scalar(dst, src, 1.0, 0.0, ALU.mult, ALU.add)
+
+        def dealt(bank):
+            return bank[:].rearrange("p (m t) -> p t m", t=PACK)
+
+        def tm(tile):
+            return tile[:].rearrange("p (t m) -> p t m", t=PACK)
+
+        def f32_tiles(name):
+            return [sb.tile([P, H], F32, name="%s%d" % (name, h)) for h in range(HALVES)]
+
+        c15, pair, gap, edge, gap2, edge2 = (f32_tiles(n) for n in ("c15", "pair", "gap", "edge", "gap2", "edge2"))
+        for h in range(HALVES):
+            nc.scalar.activation(tm(c15[h]), dealt(h_bank(2, h)), ACT.Copy, scale=1.5)
+        for h in range(HALVES):
+            nc.vector.scalar_tensor_tensor(tm(pair[h]), dealt(h_bank(1, h)), 1.5, tm(c15[h]), ALU.mult, ALU.add)
+            nc.vector.scalar_tensor_tensor(tm(gap[h]), dealt(h_bank(1, h)), 1.5, tm(c15[h]), ALU.mult, ALU.subtract)
+            nc.vector.scalar_tensor_tensor(tm(edge[h]), tm(pair[h]), -1.0 / 3.0, dealt(h_bank(0, h)), ALU.mult, ALU.add)
+            nc.scalar.activation(gap2[h][:], gap[h][:], ACT.Square, bias=zero[:], scale=1.0 / math.sqrt(3.0))
+            nc.scalar.activation(edge2[h][:], edge[h][:], ACT.Square, bias=zero[:])
+
+        w23_code = sb.tile([P, 2 * N], U32, name="w23_code", align_bytes=64)
+        w23_scale = sb.tile([P, 2 * N], U8, name="w23_scale", align_bytes=64)
+        nc.vector.quantize_mx(w23_code[:].bitcast(FP8X4), w23_scale[:], w23_grouped[:])
+
+        def turn_and_add(bank, first, second):
+            for n, tile in enumerate((first, second)):
+                for t in range(PACK):
+                    nc.tensor.matmul(
+                        bank[:, P * t : P * (t + 1)],
+                        tile[:, P * t : P * (t + 1)],
+                        ident[:],
+                        is_transpose=True,
+                        start=(n == 0 and t == 0),
+                        stop=(n == 1 and t == PACK - 1),
+                    )
+
+        def woven(bank):
+            return bank[:].rearrange("p (t v) -> p v t", t=PACK)
+
+        sum_bank = [banks[6], h_bank(2, 0)]
+        square_bank = [banks[7], h_bank(2, 1)]
+        for h in range(HALVES):
+            turn_and_add(sum_bank[h], pair[h], edge[h])
+            turn_and_add(square_bank[h], gap2[h], edge2[h])
+            stats = []
+            mean = sb.tile([P, P * PACK], BF16, name="mean%d" % h, align_bytes=64)
+            if h == 0:
+                nc.scalar.activation(mean[:].rearrange("p (v t) -> p v t", t=PACK), woven(sum_bank[h]), ACT.Copy, scale=1.0 / 3.0)
+            else:
+                nc.vector.tensor_scalar(mean[:].rearrange("p (v t) -> p v t", t=PACK), woven(sum_bank[h]), 1.0 / 3.0, None, ALU.mult)
+            dev = sb.tile([P, P * PACK], BF16, name="dev%d" % h, align_bytes=64)
+            nc.scalar.activation(dev[:].rearrange("p (v t) -> p v t", t=PACK), woven(square_bank[h]), ACT.Sqrt, bias=zero[:], scale=2.0 / 9.0)
+            for u, values in enumerate((mean, dev)):
+                code = sb.tile([P, P], U32, name="stat_code%d_%d" % (h, u), align_bytes=64)
+                scale = sb.tile([P, P], U8, name="stat_scale%d_%d" % (h, u), align_bytes=64)
+                nc.vector.quantize_mx(code[:].bitcast(FP8X4), scale[:], values[:])
+                stats.append((code, scale))
+            for u, (code, scale) in enumerate(stats):
+                for m in range(N // P):
+                    cols = slice(N * u + P * m, N * u + P * (m + 1))
+                    nc.tensor.matmul_mx(
+                        h_bank(m, h)[:, 0:P],
+                        lhsT=w23_code[:, cols].bitcast(FP8X4),
+                        lhsT_scale=w23_scale[:, cols],
+                        rhs=code[:].bitcast(FP8X4),
+                        rhs_scale=scale[:],
+                        start=(u == 0),
+                        stop=(u == 1),
+                    )
+            for m in range(N // P):
+                result = sb.tile([P, P], F32, name="result%d_%d" % (h, m))
+                if m == 0:
+                    nc.vector.tensor_copy(result[:], h_bank(m, h)[:, 0:P])
+                    nc.sync.dma_start(out[P * m : P * (m + 1), P * h : P * (h + 1)], result[:])
+                else:
+                    nc.scalar.copy(result[:], h_bank(m, h)[:, 0:P])
+                    nc.scalar.dma_start(out[P * m : P * (m + 1), P * h : P * (h + 1)], result[:])

@@ -40,29 +40,34 @@ def tile_picked_statpool_none_p_kernel(tc, x_words, x_scales, w1, w2, w3, offs, 
         offsets = sb.tile([P, S // 16], U16, name="offsets")
         nc.sync.dma_start(offsets[:], offs)
 
-        x_table = [sb.tile([P, T], U32, name="x_table%d" % g, tag="x_table%d" % g, align_bytes=64) for g in range(PASSES)]
-        w1_raw = [sb.tile([P, PACK, H], F32, name="w1_raw%d" % g, tag="raw%d" % g) for g in range(PASSES)]
+        x_table = [sb.tile([P, T], U32, name="x_table0", tag="x_table0", align_bytes=64)]
 
         def load_x(g):
             nc.sync.dma_start(x_table[g][:].bitcast(I32), x_words[g].rearrange("p n t -> p (n t)").bitcast(I32))
 
         def load_rows(raw, rows):
-            nc.sync.dma_start(raw[:], rows.rearrange("(p j) c -> p j c", j=PACK))
+            nc.sync.dma_start(raw, rows.rearrange("(p j) c -> p j c", j=PACK))
 
-        scale_table = sb.tile([P, T], U8, name="scale_table", tag="stage", align_bytes=64)
+        scale_table = sb.tile([P, T], U8, name="scale_table", align_bytes=64)
         nc.vector.memset(scale_table[:].bitcast(I32), 0)
-        zero_in = sb.tile([P, 1], F32, name="zero_in")
+        zero_in = sb.tile([P, 1], F32, name="zero_in", tag="raw")
         nc.vector.memset(zero_in[:], 0.0)
+        zero_bias = sb.tile([P, 1], F32, name="zero_bias", tag="x_table1", align_bytes=64)
+        nc.vector.memset(zero_bias[:], 0.0)
+        load_x(0)
         for q in range(4):
-            nc.gpsimd.dma_start(
+            nc.sync.dma_start(
                 scale_table[32 * q : 32 * q + 4 * PASSES, :].bitcast(I32),
                 x_scales[:, 4 * q : 4 * q + 4, :].bitcast(I32),
             )
         zero = sb.tile([P, 1], F32, name="zero")
-        nc.scalar.activation(zero[:], zero_in[:], ACT.Sqrt)
+        nc.scalar.activation(zero[:], zero_in[:], ACT.Sqrt, bias=zero_bias[:])
 
-        load_x(0)
-        load_rows(w1_raw[0], w1[0:512, :])
+        x_table.append(sb.tile([P, T], U32, name="x_table1", tag="x_table1", align_bytes=64))
+        w1_both = sb.tile([P, PASSES * PACK * H], F32, name="w1_both", tag="raw")
+        w1_raw = [w1_both[:, g * PACK * H : (g + 1) * PACK * H].rearrange("p (j c) -> p j c", j=PACK) for g in range(PASSES)]
+        load_rows(w1_raw[0][:, :, 0:256], w1[0:512, 0:256])
+        load_rows(w1_raw[0][:, :, 256:512], w1[0:512, 256:512])
         load_rows(w1_raw[1], w1[512:1024, :])
         load_x(1)
 
@@ -71,15 +76,15 @@ def tile_picked_statpool_none_p_kernel(tc, x_words, x_scales, w1, w2, w3, offs, 
 
         banks = [ps.tile([P, 512], F32, name="bank%d" % b) for b in range(8)]
 
-        x_scale = sb.tile([P, S], U8, name="x_scale", align_bytes=64)
-        nc.vector.tensor_copy(x_scale[:], scale_table[:].indirect(offsets[:]))
         x_code0 = sb.tile([P, S], U32, name="x_code0", align_bytes=64)
         nc.vector.tensor_copy(x_code0[:], x_table[0][:].indirect(offsets[:]))
+        x_scale = sb.tile([P, S], U8, name="x_scale", align_bytes=64)
+        nc.vector.tensor_copy(x_scale[:], scale_table[:].indirect(offsets[:]))
 
         w1_code, w1_scale = [], []
         for g in range(PASSES):
-            grouped = sb.tile([P, H * PACK], BF16, name="w1_grouped%d" % g, tag="stage", align_bytes=64)
-            for lo, hi, on_vector in ((0, W1_VECTOR_COLS, True), (W1_VECTOR_COLS, H, False)):
+            grouped = sb.tile([P, H * PACK], BF16, name="w1_grouped%d" % g, align_bytes=64)
+            for lo, hi, on_vector in (((0, 256, False), (256, H, False)), ((0, W1_VECTOR_COLS, True), (W1_VECTOR_COLS, H, False)))[g]:
                 dst, src = weave_views(grouped[:, PACK * lo : PACK * hi], w1_raw[g][:, :, lo:hi])
                 if on_vector:
                     nc.vector.tensor_copy(dst, src)
@@ -91,7 +96,8 @@ def tile_picked_statpool_none_p_kernel(tc, x_words, x_scales, w1, w2, w3, offs, 
             w1_code.append(code)
             w1_scale.append(scale)
 
-        w23_raw = [sb.tile([P, PACK, N], F32, name="w23_raw%d" % u, tag="raw%d" % u) for u in range(2)]
+        w23_both = sb.tile([P, 2 * PACK * N], F32, name="w23_both", tag="raw")
+        w23_raw = [w23_both[:, u * PACK * N : (u + 1) * PACK * N].rearrange("p (j c) -> p j c", j=PACK) for u in range(2)]
         load_rows(w23_raw[0], w2)
         load_rows(w23_raw[1], w3)
 
@@ -115,7 +121,7 @@ def tile_picked_statpool_none_p_kernel(tc, x_words, x_scales, w1, w2, w3, offs, 
         for d in order:
             for h in range(HALVES):
                 first_product(0, d, h, x_code0[:, V * d + P * h : V * d + P * (h + 1)])
-        x_code1 = sb.tile([P, S], U32, name="x_code1", tag="stage", align_bytes=64)
+        x_code1 = sb.tile([P, S], U32, name="x_code1", align_bytes=64)
         for d in order:
             piece = x_code1[:, V * d : V * (d + 1)]
             nc.vector.tensor_copy(piece, x_table[1][:].indirect(offsets[:, 16 * d : 16 * (d + 1)]))
@@ -124,8 +130,8 @@ def tile_picked_statpool_none_p_kernel(tc, x_words, x_scales, w1, w2, w3, offs, 
 
         w23_grouped = sb.tile([P, 2 * N * PACK], BF16, name="w23_grouped", tag="x_table1", align_bytes=64)
         for u in range(2):
-            dst, src = weave_views(w23_grouped[:, u * N * PACK : (u + 1) * N * PACK], w23_raw[u][:])
-            nc.gpsimd.tensor_scalar(dst, src, 1.0, 0.0, ALU.mult, ALU.add)
+            dst = w23_grouped[:, u * N * PACK : (u + 1) * N * PACK].rearrange("p (c j) -> p c j", j=PACK)
+            nc.gpsimd.tensor_scalar(dst, w23_raw[u].rearrange("p j c -> p c j"), 1.0, 0.0, ALU.mult, ALU.add)
 
         def dealt(bank):
             return bank[:].rearrange("p (m t) -> p t m", t=PACK)
@@ -134,7 +140,7 @@ def tile_picked_statpool_none_p_kernel(tc, x_words, x_scales, w1, w2, w3, offs, 
             return tile[:].rearrange("p (t m) -> p t m", t=PACK)
 
         def f32_tiles(name):
-            return [sb.tile([P, H], F32, name="%s%d" % (name, h)) for h in range(HALVES)]
+            return [sb.tile([P, H], F32, name="%s%d" % (name, h), align_bytes=64) for h in range(HALVES)]
 
         c15, pair, gap, edge, gap2, edge2 = (f32_tiles(n) for n in ("c15", "pair", "gap", "edge", "gap2", "edge2"))
         for h in range(HALVES):
@@ -142,11 +148,14 @@ def tile_picked_statpool_none_p_kernel(tc, x_words, x_scales, w1, w2, w3, offs, 
         for h in range(HALVES):
             nc.vector.scalar_tensor_tensor(tm(pair[h]), dealt(h_bank(1, h)), 1.5, tm(c15[h]), ALU.mult, ALU.add)
             nc.vector.scalar_tensor_tensor(tm(gap[h]), dealt(h_bank(1, h)), 1.5, tm(c15[h]), ALU.mult, ALU.subtract)
-            nc.vector.scalar_tensor_tensor(tm(edge[h]), tm(pair[h]), -1.0 / 3.0, dealt(h_bank(0, h)), ALU.mult, ALU.add)
             nc.scalar.activation(gap2[h][:], gap[h][:], ACT.Square, bias=zero[:], scale=1.0 / math.sqrt(3.0))
-            nc.scalar.activation(edge2[h][:], edge[h][:], ACT.Square, bias=zero[:])
+            for lo, hi in ((0, 4),) if h == 0 else ((0, 2), (2, 4)):
+                nc.vector.scalar_tensor_tensor(
+                    tm(edge[h])[:, lo:hi, :], tm(pair[h])[:, lo:hi, :], -1.0 / 3.0, dealt(h_bank(0, h))[:, lo:hi, :], ALU.mult, ALU.add
+                )
+                nc.scalar.activation(edge2[h][:, P * lo : P * hi], edge[h][:, P * lo : P * hi], ACT.Square, bias=zero[:])
 
-        w23_code = sb.tile([P, 2 * N], U32, name="w23_code", align_bytes=64)
+        w23_code = sb.tile([P, 2 * N], U32, name="w23_code", tag="c151", align_bytes=64)
         w23_scale = sb.tile([P, 2 * N], U8, name="w23_scale", align_bytes=64)
         nc.vector.quantize_mx(w23_code[:].bitcast(FP8X4), w23_scale[:], w23_grouped[:])
 
@@ -171,7 +180,7 @@ def tile_picked_statpool_none_p_kernel(tc, x_words, x_scales, w1, w2, w3, offs, 
             turn_and_add(sum_bank[h], pair[h], edge[h])
             turn_and_add(square_bank[h], gap2[h], edge2[h])
             stats = []
-            mean = sb.tile([P, P * PACK], BF16, name="mean%d" % h, align_bytes=64)
+            mean = sb.tile([P, P * PACK], BF16, name="mean%d" % h, tag=("mean0", "x_table1")[h], align_bytes=64)
             if h == 0:
                 nc.scalar.activation(mean[:].rearrange("p (v t) -> p v t", t=PACK), woven(sum_bank[h]), ACT.Copy, scale=1.0 / 3.0)
             else:
@@ -179,7 +188,7 @@ def tile_picked_statpool_none_p_kernel(tc, x_words, x_scales, w1, w2, w3, offs, 
             dev = sb.tile([P, P * PACK], BF16, name="dev%d" % h, align_bytes=64)
             nc.scalar.activation(dev[:].rearrange("p (v t) -> p v t", t=PACK), woven(square_bank[h]), ACT.Sqrt, bias=zero[:], scale=2.0 / 9.0)
             for u, values in enumerate((mean, dev)):
-                code = sb.tile([P, P], U32, name="stat_code%d_%d" % (h, u), align_bytes=64)
+                code = sb.tile([P, P], U32, name="stat_code%d_%d" % (h, u), tag="x_table1" if h + u == 2 else "stat_code%d_%d" % (h, u), align_bytes=64)
                 scale = sb.tile([P, P], U8, name="stat_scale%d_%d" % (h, u), align_bytes=64)
                 nc.vector.quantize_mx(code[:].bitcast(FP8X4), scale[:], values[:])
                 stats.append((code, scale))
@@ -197,9 +206,9 @@ def tile_picked_statpool_none_p_kernel(tc, x_words, x_scales, w1, w2, w3, offs, 
                     )
             for m in range(N // P):
                 result = sb.tile([P, P], F32, name="result%d_%d" % (h, m))
-                if m == 0:
+                if m == 0 and h == 1:
                     nc.vector.tensor_copy(result[:], h_bank(m, h)[:, 0:P])
-                    nc.sync.dma_start(out[P * m : P * (m + 1), P * h : P * (h + 1)], result[:])
                 else:
                     nc.scalar.copy(result[:], h_bank(m, h)[:, 0:P])
-                    nc.scalar.dma_start(out[P * m : P * (m + 1), P * h : P * (h + 1)], result[:])
+                queue = nc.scalar if m == 1 and h == 1 else nc.sync
+                queue.dma_start(out[P * m : P * (m + 1), P * h : P * (h + 1)], result[:])

@@ -38,7 +38,6 @@ def tile_picked_statpool_none_p_kernel(tc, x_words, x_scales, w1, w2, w3, offs, 
         ps = ctx.enter_context(tc.psum_pool(name="ps", bufs=1))
 
         offsets = sb.tile([P, S // 16], U16, name="offsets")
-        nc.sync.dma_start(offsets[:], offs)
 
         x_table = [sb.tile([P, T], U32, name="x_table0", tag="x_table0", align_bytes=64)]
 
@@ -55,16 +54,19 @@ def tile_picked_statpool_none_p_kernel(tc, x_words, x_scales, w1, w2, w3, offs, 
         zero_bias = sb.tile([P, 1], F32, name="zero_bias", tag="x_table1", align_bytes=64)
         nc.vector.memset(zero_bias[:], 0.0)
         load_x(0)
+        nc.sync.dma_start(offsets[:], offs)
         for q in range(4):
             nc.sync.dma_start(
                 scale_table[32 * q : 32 * q + 4 * PASSES, :].bitcast(I32),
                 x_scales[:, 4 * q : 4 * q + 4, :].bitcast(I32),
             )
         zero = sb.tile([P, 1], F32, name="zero")
-        nc.scalar.activation(zero[:], zero_in[:], ACT.Sqrt, bias=zero_bias[:])
+        seed = sb.tile([P, 1], F32, name="seed")
+        nc.vector.tensor_tensor(seed[:], zero_in[:], zero_bias[:], ALU.add)
+        nc.scalar.activation(zero[:], seed[:], ACT.Sqrt)
 
         x_table.append(sb.tile([P, T], U32, name="x_table1", tag="x_table1", align_bytes=64))
-        w1_both = sb.tile([P, PASSES * PACK * H], F32, name="w1_both", tag="raw")
+        w1_both = sb.tile([P, PASSES * PACK * H + 2 * PACK * N], F32, name="w1_both", tag="raw")
         w1_raw = [w1_both[:, g * PACK * H : (g + 1) * PACK * H].rearrange("p (j c) -> p j c", j=PACK) for g in range(PASSES)]
         load_rows(w1_raw[0][:, :, 0:256], w1[0:512, 0:256])
         load_rows(w1_raw[0][:, :, 256:512], w1[0:512, 256:512])
@@ -96,7 +98,7 @@ def tile_picked_statpool_none_p_kernel(tc, x_words, x_scales, w1, w2, w3, offs, 
             w1_code.append(code)
             w1_scale.append(scale)
 
-        w23_both = sb.tile([P, 2 * PACK * N], F32, name="w23_both", tag="raw")
+        w23_both = w1_both[:, PASSES * PACK * H :]
         w23_raw = [w23_both[:, u * PACK * N : (u + 1) * PACK * N].rearrange("p (j c) -> p j c", j=PACK) for u in range(2)]
         load_rows(w23_raw[0], w2)
         load_rows(w23_raw[1], w3)
@@ -129,9 +131,9 @@ def tile_picked_statpool_none_p_kernel(tc, x_words, x_scales, w1, w2, w3, offs, 
                 first_product(1, d, h, piece[:, P * h : P * (h + 1)])
 
         w23_grouped = sb.tile([P, 2 * N * PACK], BF16, name="w23_grouped", tag="x_table1", align_bytes=64)
-        for u in range(2):
-            dst = w23_grouped[:, u * N * PACK : (u + 1) * N * PACK].rearrange("p (c j) -> p c j", j=PACK)
-            nc.gpsimd.tensor_scalar(dst, w23_raw[u].rearrange("p j c -> p c j"), 1.0, 0.0, ALU.mult, ALU.add)
+        for u, hi in ((0, N), (1, N // 2)):
+            dst = w23_grouped[:, u * N * PACK : (u * N + hi) * PACK].rearrange("p (c j) -> p c j", j=PACK)
+            nc.gpsimd.tensor_scalar(dst, w23_raw[u][:, :, 0:hi].rearrange("p j c -> p c j"), 1.0, 0.0, ALU.mult, ALU.add)
 
         def dealt(bank):
             return bank[:].rearrange("p (m t) -> p t m", t=PACK)
@@ -155,7 +157,9 @@ def tile_picked_statpool_none_p_kernel(tc, x_words, x_scales, w1, w2, w3, offs, 
                 )
                 nc.scalar.activation(edge2[h][:, P * lo : P * hi], edge[h][:, P * lo : P * hi], ACT.Square, bias=zero[:])
 
-        w23_code = sb.tile([P, 2 * N], U32, name="w23_code", tag="c151", align_bytes=64)
+        dst, src = weave_views(w23_grouped[:, (N + N // 2) * PACK :], w23_raw[1][:, :, N // 2 : N])
+        nc.scalar.copy(dst, src)
+        w23_code = sb.tile([P, 2 * N], U32, name="w23_code", tag="pair1", align_bytes=64)
         w23_scale = sb.tile([P, 2 * N], U8, name="w23_scale", align_bytes=64)
         nc.vector.quantize_mx(w23_code[:].bitcast(FP8X4), w23_scale[:], w23_grouped[:])
 
@@ -185,7 +189,7 @@ def tile_picked_statpool_none_p_kernel(tc, x_words, x_scales, w1, w2, w3, offs, 
                 nc.scalar.activation(mean[:].rearrange("p (v t) -> p v t", t=PACK), woven(sum_bank[h]), ACT.Copy, scale=1.0 / 3.0)
             else:
                 nc.vector.tensor_scalar(mean[:].rearrange("p (v t) -> p v t", t=PACK), woven(sum_bank[h]), 1.0 / 3.0, None, ALU.mult)
-            dev = sb.tile([P, P * PACK], BF16, name="dev%d" % h, align_bytes=64)
+            dev = sb.tile([P, P * PACK], BF16, name="dev%d" % h, tag=("edge1", "dev1")[h], align_bytes=64)
             nc.scalar.activation(dev[:].rearrange("p (v t) -> p v t", t=PACK), woven(square_bank[h]), ACT.Sqrt, bias=zero[:], scale=2.0 / 9.0)
             for u, values in enumerate((mean, dev)):
                 code = sb.tile([P, P], U32, name="stat_code%d_%d" % (h, u), tag="x_table1" if h + u == 2 else "stat_code%d_%d" % (h, u), align_bytes=64)

@@ -22,12 +22,12 @@ PACK = 4
 PASSES = K // (P * PACK)
 HALVES = V // P
 PIECES = S // V
-W1_VECTOR_COLS = 344
+W1_VECTOR_COLS = 320
 
 
 def weave_views(grouped, raw):
-    dst = grouped.rearrange("p (c i j) -> p c j i", i=PACK, j=PACK)
-    src = raw.rearrange("p j (c i) -> p c j i", i=PACK)
+    dst = grouped.rearrange("p (c j) -> p c j", j=PACK)
+    src = raw.rearrange("p j c -> p c j")
     return dst, src
 
 
@@ -86,7 +86,7 @@ def tile_picked_statpool_none_p_kernel(tc, x_words, x_scales, w1, w2, w3, offs, 
         w1_code, w1_scale = [], []
         for g in range(PASSES):
             grouped = sb.tile([P, H * PACK], BF16, name="w1_grouped%d" % g, align_bytes=64)
-            for lo, hi, on_vector in (((0, 256, False), (256, H, False)), ((0, W1_VECTOR_COLS, True), (W1_VECTOR_COLS, H, False)))[g]:
+            for lo, hi, on_vector in (((0, 256, False), (256, 416, False), (416, H, True)), ((0, W1_VECTOR_COLS, True), (W1_VECTOR_COLS, H, False)))[g]:
                 dst, src = weave_views(grouped[:, PACK * lo : PACK * hi], w1_raw[g][:, :, lo:hi])
                 if on_vector:
                     nc.vector.tensor_copy(dst, src)
@@ -106,7 +106,7 @@ def tile_picked_statpool_none_p_kernel(tc, x_words, x_scales, w1, w2, w3, offs, 
         order = (2, 1, 0)
 
         def h_bank(d, h):
-            return banks[2 * d + h]
+            return banks[2 * d + h] if (d, h) != (0, 1) else banks[2]
 
         def first_product(g, d, h, codes):
             lo = V * d + P * h
@@ -121,13 +121,13 @@ def tile_picked_statpool_none_p_kernel(tc, x_words, x_scales, w1, w2, w3, offs, 
             )
 
         for d in order:
-            for h in range(HALVES):
+            for h in range(HALVES if d > 0 else 1):
                 first_product(0, d, h, x_code0[:, V * d + P * h : V * d + P * (h + 1)])
         x_code1 = sb.tile([P, S], U32, name="x_code1", align_bytes=64)
         for d in order:
             piece = x_code1[:, V * d : V * (d + 1)]
             nc.vector.tensor_copy(piece, x_table[1][:].indirect(offsets[:, 16 * d : 16 * (d + 1)]))
-            for h in range(HALVES):
+            for h in range(HALVES if d > 0 else 1):
                 first_product(1, d, h, piece[:, P * h : P * (h + 1)])
 
         w23_grouped = sb.tile([P, 2 * N * PACK], BF16, name="w23_grouped", tag="x_table1", align_bytes=64)
@@ -150,6 +150,9 @@ def tile_picked_statpool_none_p_kernel(tc, x_words, x_scales, w1, w2, w3, offs, 
         for h in range(HALVES):
             nc.vector.scalar_tensor_tensor(tm(pair[h]), dealt(h_bank(1, h)), 1.5, tm(c15[h]), ALU.mult, ALU.add)
             nc.vector.scalar_tensor_tensor(tm(gap[h]), dealt(h_bank(1, h)), 1.5, tm(c15[h]), ALU.mult, ALU.subtract)
+            if h == 0:
+                first_product(0, 0, 1, x_code0[:, P : 2 * P])
+                first_product(1, 0, 1, x_code1[:, P : 2 * P])
             nc.scalar.activation(gap2[h][:], gap[h][:], ACT.Square, bias=zero[:], scale=1.0 / math.sqrt(3.0))
             for lo, hi in ((0, 4),) if h == 0 else ((0, 2), (2, 4)):
                 nc.vector.scalar_tensor_tensor(
@@ -178,6 +181,7 @@ def tile_picked_statpool_none_p_kernel(tc, x_words, x_scales, w1, w2, w3, offs, 
         def woven(bank):
             return bank[:].rearrange("p (t v) -> p v t", t=PACK)
 
+        out_bank = [[banks[1], banks[0]], [banks[2], banks[3]]]
         sum_bank = [banks[6], h_bank(2, 0)]
         square_bank = [banks[7], h_bank(2, 1)]
         for h in range(HALVES):
@@ -200,7 +204,7 @@ def tile_picked_statpool_none_p_kernel(tc, x_words, x_scales, w1, w2, w3, offs, 
                 for m in range(N // P):
                     cols = slice(N * u + P * m, N * u + P * (m + 1))
                     nc.tensor.matmul_mx(
-                        h_bank(m, h)[:, 0:P],
+                        out_bank[h][m][:, 0:P],
                         lhsT=w23_code[:, cols].bitcast(FP8X4),
                         lhsT_scale=w23_scale[:, cols],
                         rhs=code[:].bitcast(FP8X4),
@@ -211,8 +215,8 @@ def tile_picked_statpool_none_p_kernel(tc, x_words, x_scales, w1, w2, w3, offs, 
             for m in range(N // P):
                 result = sb.tile([P, P], F32, name="result%d_%d" % (h, m))
                 if m == 0 and h == 1:
-                    nc.vector.tensor_copy(result[:], h_bank(m, h)[:, 0:P])
+                    nc.vector.tensor_copy(result[:], out_bank[h][m][:, 0:P])
                 else:
-                    nc.scalar.copy(result[:], h_bank(m, h)[:, 0:P])
+                    nc.scalar.copy(result[:], out_bank[h][m][:, 0:P])
                 queue = nc.scalar if m == 1 and h == 1 else nc.sync
                 queue.dma_start(out[P * m : P * (m + 1), P * h : P * (h + 1)], result[:])

@@ -19,16 +19,20 @@ ACT = mybir.ActivationFunctionType
 
 P = 128
 PACK = 4
-PASSES = K // (P * PACK)
+K_PASS = P * PACK
+PASSES = K // K_PASS
 HALVES = V // P
-PIECES = S // V
-W1_VECTOR_COLS = 320
+QUADRANT = 32
+LIST_COLS = V // 16
+ALIGN = 64
+A, B, C = 0, 1, 2
+
+W1_SCALAR_COLS = (288, 192)
+W3_GPSIMD_COLS = N // 2
 
 
-def weave_views(grouped, raw):
-    dst = grouped.rearrange("p (c j) -> p c j", j=PACK)
-    src = raw.rearrange("p j c -> p c j")
-    return dst, src
+def four_rows_side_by_side(rounded, raw):
+    return rounded.rearrange("p (c j) -> p c j", j=PACK), raw.rearrange("p j c -> p c j")
 
 
 def tile_picked_statpool_none_p_kernel(tc, x_words, x_scales, w1, w2, w3, offs, out):
@@ -37,134 +41,145 @@ def tile_picked_statpool_none_p_kernel(tc, x_words, x_scales, w1, w2, w3, offs, 
         sb = ctx.enter_context(tc.tile_pool(name="sb", bufs=1))
         ps = ctx.enter_context(tc.psum_pool(name="ps", bufs=1))
 
-        offsets = sb.tile([P, S // 16], U16, name="offsets")
-
-        x_table = [sb.tile([P, T], U32, name="x_table0", tag="x_table0", align_bytes=64)]
-
-        def load_x(g):
-            nc.sync.dma_start(x_table[g][:].bitcast(I32), x_words[g].rearrange("p n t -> p (n t)").bitcast(I32))
+        def load_words(table, g):
+            nc.sync.dma_start(table[:].bitcast(I32), x_words[g].rearrange("p n t -> p (n t)").bitcast(I32))
 
         def load_rows(raw, rows):
             nc.sync.dma_start(raw, rows.rearrange("(p j) c -> p j c", j=PACK))
 
-        scale_table = sb.tile([P, T], U8, name="scale_table", align_bytes=64)
+        def quantize(name, values, width, code_tag):
+            code = sb.tile([P, width], U32, name=name + "_code", tag=code_tag, align_bytes=ALIGN)
+            scale = sb.tile([P, width], U8, name=name + "_scale", align_bytes=ALIGN)
+            nc.vector.quantize_mx(code[:].bitcast(FP8X4), scale[:], values[:])
+            return code, scale
+
+        offsets = sb.tile([P, S // 16], U16, name="offsets")
+        word_table0 = sb.tile([P, T], U32, name="word_table0", align_bytes=ALIGN)
+
+        scale_table = sb.tile([P, T], U8, name="scale_table", align_bytes=ALIGN)
         nc.vector.memset(scale_table[:].bitcast(I32), 0)
-        zero_in = sb.tile([P, 1], F32, name="zero_in", tag="raw")
-        nc.vector.memset(zero_in[:], 0.0)
-        zero_bias = sb.tile([P, 1], F32, name="zero_bias", tag="x_table1", align_bytes=64)
-        nc.vector.memset(zero_bias[:], 0.0)
-        load_x(0)
+        zero_a = sb.tile([P, 1], F32, name="zero_a", tag="weights")
+        nc.vector.memset(zero_a[:], 0.0)
+        zero_b = sb.tile([P, 1], F32, name="zero_b", tag="late", align_bytes=ALIGN)
+        nc.vector.memset(zero_b[:], 0.0)
+
+        load_words(word_table0, 0)
         nc.sync.dma_start(offsets[:], offs)
-        for q in range(4):
+        for q in range(P // QUADRANT):
             nc.sync.dma_start(
-                scale_table[32 * q : 32 * q + 4 * PASSES, :].bitcast(I32),
-                x_scales[:, 4 * q : 4 * q + 4, :].bitcast(I32),
+                scale_table[QUADRANT * q : QUADRANT * q + PACK * PASSES, :].bitcast(I32),
+                x_scales[:, PACK * q : PACK * (q + 1), :].bitcast(I32),
             )
+
         zero = sb.tile([P, 1], F32, name="zero")
-        seed = sb.tile([P, 1], F32, name="seed")
-        nc.vector.tensor_tensor(seed[:], zero_in[:], zero_bias[:], ALU.add)
-        nc.scalar.activation(zero[:], seed[:], ACT.Sqrt)
+        zero_sum = sb.tile([P, 1], F32, name="zero_sum")
+        nc.vector.tensor_tensor(zero_sum[:], zero_a[:], zero_b[:], ALU.add)
+        nc.scalar.activation(zero[:], zero_sum[:], ACT.Sqrt)
 
-        x_table.append(sb.tile([P, T], U32, name="x_table1", tag="x_table1", align_bytes=64))
-        w1_both = sb.tile([P, PASSES * PACK * H + 2 * PACK * N], F32, name="w1_both", tag="raw")
-        w1_raw = [w1_both[:, g * PACK * H : (g + 1) * PACK * H].rearrange("p (j c) -> p j c", j=PACK) for g in range(PASSES)]
-        load_rows(w1_raw[0][:, :, 0:256], w1[0:512, 0:256])
-        load_rows(w1_raw[0][:, :, 256:512], w1[0:512, 256:512])
-        load_rows(w1_raw[1], w1[512:1024, :])
-        load_x(1)
+        word_table1 = sb.tile([P, T], U32, name="word_table1", tag="late", align_bytes=ALIGN)
+        weights = sb.tile([P, PACK * (PASSES * H + 2 * N)], F32, name="weights", tag="weights")
 
-        ident = sb.tile([P, P], F32, name="ident")
-        make_identity(nc, ident[:])
+        def raw_rows(first, width):
+            return weights[:, PACK * first : PACK * (first + width)].rearrange("p (j c) -> p j c", j=PACK)
 
-        banks = [ps.tile([P, 512], F32, name="bank%d" % b) for b in range(8)]
+        w1_raw = [raw_rows(g * H, H) for g in range(PASSES)]
+        w2_raw, w3_raw = raw_rows(PASSES * H, N), raw_rows(PASSES * H + N, N)
+        for g in range(PASSES):
+            load_rows(w1_raw[g], w1[K_PASS * g : K_PASS * (g + 1), :])
+        load_words(word_table1, 1)
 
-        x_code0 = sb.tile([P, S], U32, name="x_code0", align_bytes=64)
-        nc.vector.tensor_copy(x_code0[:], x_table[0][:].indirect(offsets[:]))
-        x_scale = sb.tile([P, S], U8, name="x_scale", align_bytes=64)
+        identity = sb.tile([P, P], F32, name="identity")
+        make_identity(nc, identity[:])
+
+        banks = [ps.tile([P, K_PASS], F32, name="bank%d" % b) for b in range(8)]
+
+        x_code0 = sb.tile([P, S], U32, name="x_code0", align_bytes=ALIGN)
+        nc.vector.tensor_copy(x_code0[:], word_table0[:].indirect(offsets[:]))
+        x_scale = sb.tile([P, S], U8, name="x_scale", align_bytes=ALIGN)
         nc.vector.tensor_copy(x_scale[:], scale_table[:].indirect(offsets[:]))
 
-        w1_code, w1_scale = [], []
+        w1_mx = []
         for g in range(PASSES):
-            grouped = sb.tile([P, H * PACK], BF16, name="w1_grouped%d" % g, align_bytes=64)
-            for lo, hi, on_vector in (((0, 256, False), (256, 416, False), (416, H, True)), ((0, W1_VECTOR_COLS, True), (W1_VECTOR_COLS, H, False)))[g]:
-                dst, src = weave_views(grouped[:, PACK * lo : PACK * hi], w1_raw[g][:, :, lo:hi])
-                if on_vector:
-                    nc.vector.tensor_copy(dst, src)
-                else:
-                    nc.scalar.copy(dst, src)
-            code = sb.tile([P, H], U32, name="w1_code%d" % g, align_bytes=64)
-            scale = sb.tile([P, H], U8, name="w1_scale%d" % g, align_bytes=64)
-            nc.vector.quantize_mx(code[:].bitcast(FP8X4), scale[:], grouped[:])
-            w1_code.append(code)
-            w1_scale.append(scale)
+            w1_rounded = sb.tile([P, H * PACK], BF16, name="w1_rounded%d" % g, align_bytes=ALIGN)
+            split = W1_SCALAR_COLS[g]
+            nc.scalar.copy(*four_rows_side_by_side(w1_rounded[:, : PACK * split], w1_raw[g][:, :, :split]))
+            nc.vector.tensor_copy(*four_rows_side_by_side(w1_rounded[:, PACK * split :], w1_raw[g][:, :, split:]))
+            w1_mx.append(quantize("w1_%d" % g, w1_rounded, H, "w1_code%d" % g))
 
-        w23_both = w1_both[:, PASSES * PACK * H :]
-        w23_raw = [w23_both[:, u * PACK * N : (u + 1) * PACK * N].rearrange("p (j c) -> p j c", j=PACK) for u in range(2)]
-        load_rows(w23_raw[0], w2)
-        load_rows(w23_raw[1], w3)
+        load_rows(w2_raw, w2)
+        load_rows(w3_raw, w3)
 
-        order = (2, 1, 0)
+        h_bank = [[banks[7], banks[2]], [banks[2], banks[1]], [banks[0], banks[1]]]
+        early = ((C, 0), (C, 1), (B, 0), (A, 0))
+        x_code1 = sb.tile([P, S], U32, name="x_code1", align_bytes=ALIGN)
+        x_code = (x_code0, x_code1)
 
-        def h_bank(d, h):
-            return banks[2 * d + h] if (d, h) != (0, 1) else banks[2]
-
-        def first_product(g, d, h, codes):
-            lo = V * d + P * h
+        def first_product(g, d, h):
+            frames = slice(V * d + P * h, V * d + P * (h + 1))
             nc.tensor.matmul_mx(
-                h_bank(d, h)[:],
-                lhsT=codes.bitcast(FP8X4),
-                lhsT_scale=x_scale[4 * g : P, lo : lo + P],
-                rhs=w1_code[g][:].bitcast(FP8X4),
-                rhs_scale=w1_scale[g][:],
+                h_bank[d][h][:],
+                lhsT=x_code[g][:, frames].bitcast(FP8X4),
+                lhsT_scale=x_scale[PACK * g : P, frames],
+                rhs=w1_mx[g][0][:].bitcast(FP8X4),
+                rhs_scale=w1_mx[g][1][:],
                 start=(g == 0),
                 stop=(g == PASSES - 1),
             )
 
-        for d in order:
-            for h in range(HALVES if d > 0 else 1):
-                first_product(0, d, h, x_code0[:, V * d + P * h : V * d + P * (h + 1)])
-        x_code1 = sb.tile([P, S], U32, name="x_code1", align_bytes=64)
-        for d in order:
-            piece = x_code1[:, V * d : V * (d + 1)]
-            nc.vector.tensor_copy(piece, x_table[1][:].indirect(offsets[:, 16 * d : 16 * (d + 1)]))
-            for h in range(HALVES if d > 0 else 1):
-                first_product(1, d, h, piece[:, P * h : P * (h + 1)])
+        def both_passes(d, h):
+            for g in range(PASSES):
+                first_product(g, d, h)
 
-        w23_grouped = sb.tile([P, 2 * N * PACK], BF16, name="w23_grouped", tag="x_table1", align_bytes=64)
-        for u, hi in ((0, N), (1, N // 2)):
-            dst = w23_grouped[:, u * N * PACK : (u * N + hi) * PACK].rearrange("p (c j) -> p c j", j=PACK)
-            nc.gpsimd.tensor_scalar(dst, w23_raw[u][:, :, 0:hi].rearrange("p j c -> p c j"), 1.0, 0.0, ALU.mult, ALU.add)
+        for d, h in early:
+            first_product(0, d, h)
+        for d in (C, B, A):
+            piece = offsets[:, LIST_COLS * d : LIST_COLS * (d + 1)]
+            nc.vector.tensor_copy(x_code1[:, V * d : V * (d + 1)], word_table1[:].indirect(piece))
+            for h in range(HALVES):
+                if (d, h) in early:
+                    first_product(1, d, h)
+
+        w23_rounded = sb.tile([P, 2 * N * PACK], BF16, name="w23_rounded", tag="late", align_bytes=ALIGN)
+        w3_split = PACK * (N + W3_GPSIMD_COLS)
+        for rounded, raw in (
+            (w23_rounded[:, : PACK * N], w2_raw),
+            (w23_rounded[:, PACK * N : w3_split], w3_raw[:, :, :W3_GPSIMD_COLS]),
+        ):
+            nc.gpsimd.tensor_scalar(*four_rows_side_by_side(rounded, raw), 1.0, 0.0, ALU.mult, ALU.add)
 
         def dealt(bank):
             return bank[:].rearrange("p (m t) -> p t m", t=PACK)
 
-        def tm(tile):
+        def by_t(tile):
             return tile[:].rearrange("p (t m) -> p t m", t=PACK)
 
-        def f32_tiles(name):
-            return [sb.tile([P, H], F32, name="%s%d" % (name, h), align_bytes=64) for h in range(HALVES)]
+        def term(name):
+            return [sb.tile([P, H], F32, name="%s%d" % (name, h), align_bytes=ALIGN) for h in range(HALVES)]
 
-        c15, pair, gap, edge, gap2, edge2 = (f32_tiles(n) for n in ("c15", "pair", "gap", "edge", "gap2", "edge2"))
+        c_scaled, pair, gap, edge, gap_sq, edge_sq = (term(n) for n in ("c_scaled", "pair", "gap", "edge", "gap_sq", "edge_sq"))
         for h in range(HALVES):
-            nc.scalar.activation(tm(c15[h]), dealt(h_bank(2, h)), ACT.Copy, scale=1.5)
+            nc.scalar.activation(by_t(c_scaled[h]), dealt(h_bank[C][h]), ACT.Copy, scale=1.5)
+        both_passes(B, 1)
         for h in range(HALVES):
-            nc.vector.scalar_tensor_tensor(tm(pair[h]), dealt(h_bank(1, h)), 1.5, tm(c15[h]), ALU.mult, ALU.add)
-            nc.vector.scalar_tensor_tensor(tm(gap[h]), dealt(h_bank(1, h)), 1.5, tm(c15[h]), ALU.mult, ALU.subtract)
+            b_values = dealt(h_bank[B][h])
+            nc.vector.scalar_tensor_tensor(by_t(pair[h]), b_values, 1.5, by_t(c_scaled[h]), ALU.mult, ALU.add)
+            nc.vector.scalar_tensor_tensor(by_t(gap[h]), b_values, 1.5, by_t(c_scaled[h]), ALU.mult, ALU.subtract)
             if h == 0:
-                first_product(0, 0, 1, x_code0[:, P : 2 * P])
-                first_product(1, 0, 1, x_code1[:, P : 2 * P])
-            nc.scalar.activation(gap2[h][:], gap[h][:], ACT.Square, bias=zero[:], scale=1.0 / math.sqrt(3.0))
-            for lo, hi in ((0, 4),) if h == 0 else ((0, 2), (2, 4)):
+                both_passes(A, 1)
+            nc.scalar.activation(gap_sq[h][:], gap[h][:], ACT.Square, bias=zero[:], scale=1.0 / math.sqrt(3.0))
+            for lo, hi in ((0, PACK),) if h == 0 else ((0, PACK // 2), (PACK // 2, PACK)):
                 nc.vector.scalar_tensor_tensor(
-                    tm(edge[h])[:, lo:hi, :], tm(pair[h])[:, lo:hi, :], -1.0 / 3.0, dealt(h_bank(0, h))[:, lo:hi, :], ALU.mult, ALU.add
+                    by_t(edge[h])[:, lo:hi, :],
+                    by_t(pair[h])[:, lo:hi, :],
+                    -1.0 / 3.0,
+                    dealt(h_bank[A][h])[:, lo:hi, :],
+                    ALU.mult,
+                    ALU.add,
                 )
-                nc.scalar.activation(edge2[h][:, P * lo : P * hi], edge[h][:, P * lo : P * hi], ACT.Square, bias=zero[:])
+                nc.scalar.activation(edge_sq[h][:, P * lo : P * hi], edge[h][:, P * lo : P * hi], ACT.Square, bias=zero[:])
 
-        dst, src = weave_views(w23_grouped[:, (N + N // 2) * PACK :], w23_raw[1][:, :, N // 2 : N])
-        nc.scalar.copy(dst, src)
-        w23_code = sb.tile([P, 2 * N], U32, name="w23_code", tag="pair1", align_bytes=64)
-        w23_scale = sb.tile([P, 2 * N], U8, name="w23_scale", align_bytes=64)
-        nc.vector.quantize_mx(w23_code[:].bitcast(FP8X4), w23_scale[:], w23_grouped[:])
+        nc.scalar.copy(*four_rows_side_by_side(w23_rounded[:, w3_split:], w3_raw[:, :, W3_GPSIMD_COLS:]))
+        w23_code, w23_scale = quantize("w23", w23_rounded, 2 * N, "pair1")
 
         def turn_and_add(bank, first, second):
             for n, tile in enumerate((first, second)):
@@ -172,34 +187,35 @@ def tile_picked_statpool_none_p_kernel(tc, x_words, x_scales, w1, w2, w3, offs, 
                     nc.tensor.matmul(
                         bank[:, P * t : P * (t + 1)],
                         tile[:, P * t : P * (t + 1)],
-                        ident[:],
+                        identity[:],
                         is_transpose=True,
                         start=(n == 0 and t == 0),
                         stop=(n == 1 and t == PACK - 1),
                     )
 
-        def woven(bank):
-            return bank[:].rearrange("p (t v) -> p v t", t=PACK)
+        def four_t_side_by_side(rounded, bank):
+            return rounded[:].rearrange("p (v t) -> p v t", t=PACK), bank[:].rearrange("p (t v) -> p v t", t=PACK)
 
-        out_bank = [[banks[1], banks[0]], [banks[2], banks[3]]]
-        sum_bank = [banks[6], h_bank(2, 0)]
-        square_bank = [banks[7], h_bank(2, 1)]
+        sum_bank = [banks[3], banks[5]]
+        square_bank = [banks[4], banks[6]]
+        out_bank = [[banks[0], banks[7]], [banks[1], banks[3]]]
+        mean_tag = ("mean0", "late")
+        dev_tag = ("edge1", "dev1")
+        mean_code_tag = ("edge_sq1", "mean_code1")
+        dev_code_tag = ("dev_code0", "late")
         for h in range(HALVES):
             turn_and_add(sum_bank[h], pair[h], edge[h])
-            turn_and_add(square_bank[h], gap2[h], edge2[h])
-            stats = []
-            mean = sb.tile([P, P * PACK], BF16, name="mean%d" % h, tag=("mean0", "x_table1")[h], align_bytes=64)
+            turn_and_add(square_bank[h], gap_sq[h], edge_sq[h])
+
+            mean = sb.tile([P, P * PACK], BF16, name="mean%d" % h, tag=mean_tag[h], align_bytes=ALIGN)
             if h == 0:
-                nc.scalar.activation(mean[:].rearrange("p (v t) -> p v t", t=PACK), woven(sum_bank[h]), ACT.Copy, scale=1.0 / 3.0)
+                nc.scalar.activation(*four_t_side_by_side(mean, sum_bank[h]), ACT.Copy, scale=1.0 / 3.0)
             else:
-                nc.vector.tensor_scalar(mean[:].rearrange("p (v t) -> p v t", t=PACK), woven(sum_bank[h]), 1.0 / 3.0, None, ALU.mult)
-            dev = sb.tile([P, P * PACK], BF16, name="dev%d" % h, tag=("edge1", "dev1")[h], align_bytes=64)
-            nc.scalar.activation(dev[:].rearrange("p (v t) -> p v t", t=PACK), woven(square_bank[h]), ACT.Sqrt, bias=zero[:], scale=2.0 / 9.0)
-            for u, values in enumerate((mean, dev)):
-                code = sb.tile([P, P], U32, name="stat_code%d_%d" % (h, u), tag="x_table1" if h + u == 2 else "stat_code%d_%d" % (h, u), align_bytes=64)
-                scale = sb.tile([P, P], U8, name="stat_scale%d_%d" % (h, u), align_bytes=64)
-                nc.vector.quantize_mx(code[:].bitcast(FP8X4), scale[:], values[:])
-                stats.append((code, scale))
+                nc.vector.tensor_scalar(*four_t_side_by_side(mean, sum_bank[h]), 1.0 / 3.0, None, ALU.mult)
+            dev = sb.tile([P, P * PACK], BF16, name="dev%d" % h, tag=dev_tag[h], align_bytes=ALIGN)
+            nc.scalar.activation(*four_t_side_by_side(dev, square_bank[h]), ACT.Sqrt, bias=zero[:], scale=2.0 / 9.0)
+            stats = (quantize("mean_mx%d" % h, mean, P, mean_code_tag[h]), quantize("dev_mx%d" % h, dev, P, dev_code_tag[h]))
+
             for u, (code, scale) in enumerate(stats):
                 for m in range(N // P):
                     cols = slice(N * u + P * m, N * u + P * (m + 1))
@@ -212,11 +228,12 @@ def tile_picked_statpool_none_p_kernel(tc, x_words, x_scales, w1, w2, w3, offs, 
                         start=(u == 0),
                         stop=(u == 1),
                     )
+
             for m in range(N // P):
                 result = sb.tile([P, P], F32, name="result%d_%d" % (h, m))
-                if m == 0 and h == 1:
+                if h == 1 and m == 0:
                     nc.vector.tensor_copy(result[:], out_bank[h][m][:, 0:P])
                 else:
                     nc.scalar.copy(result[:], out_bank[h][m][:, 0:P])
-                queue = nc.scalar if m == 1 and h == 1 else nc.sync
+                queue = nc.scalar if h == 1 and m == 1 else nc.sync
                 queue.dma_start(out[P * m : P * (m + 1), P * h : P * (h + 1)], result[:])

import math
from contextlib import ExitStack

import concourse.mybir as mybir
from concourse.masks import make_identity

K, T, S, V, H, N = 1024, 2048, 768, 256, 512, 256
FLOPS = 2 * K * H * S + 2 * 2 * H * N * V

F32 = mybir.dt.float32
BF16 = mybir.dt.bfloat16
I32 = mybir.dt.int32
U32 = mybir.dt.uint32
U16 = mybir.dt.uint16
U8 = mybir.dt.uint8
FP8X4 = mybir.dt.float8_e4m3fn_x4
ALU = mybir.AluOpType
ACT = mybir.ActivationFunctionType

P = 128
PACK = 4
K_PASS = P * PACK
PASSES = K // K_PASS
HALVES = V // P
QUADRANT = 32
LIST_COLS = V // 16
ALIGN = 64
A, B, C = 0, 1, 2

W1_SCALAR_COLS = (288, 192)
W3_GPSIMD_COLS = N // 2


def four_rows_side_by_side(rounded, raw):
    return rounded.rearrange("p (c j) -> p c j", j=PACK), raw.rearrange("p j c -> p c j")


def tile_picked_statpool_none_p_kernel(tc, x_words, x_scales, w1, w2, w3, offs, out):
    nc = tc.nc
    with ExitStack() as ctx:
        sb = ctx.enter_context(tc.tile_pool(name="sb", bufs=1))
        ps = ctx.enter_context(tc.psum_pool(name="ps", bufs=1))

        def load_words(table, g):
            nc.sync.dma_start(table[:].bitcast(I32), x_words[g].rearrange("p n t -> p (n t)").bitcast(I32))

        def load_rows(raw, rows):
            nc.sync.dma_start(raw, rows.rearrange("(p j) c -> p j c", j=PACK))

        def quantize(name, values, width, code_tag):
            code = sb.tile([P, width], U32, name=name + "_code", tag=code_tag, align_bytes=ALIGN)
            scale = sb.tile([P, width], U8, name=name + "_scale", align_bytes=ALIGN)
            nc.vector.quantize_mx(code[:].bitcast(FP8X4), scale[:], values[:])
            return code, scale

        offsets = sb.tile([P, S // 16], U16, name="offsets")
        word_table0 = sb.tile([P, T], U32, name="word_table0", align_bytes=ALIGN)

        scale_table = sb.tile([P, T], U8, name="scale_table", align_bytes=ALIGN)
        nc.vector.memset(scale_table[:].bitcast(I32), 0)
        zero_a = sb.tile([P, 1], F32, name="zero_a", tag="weights")
        nc.vector.memset(zero_a[:], 0.0)
        zero_b = sb.tile([P, 1], F32, name="zero_b", tag="late", align_bytes=ALIGN)
        nc.vector.memset(zero_b[:], 0.0)

        load_words(word_table0, 0)
        nc.sync.dma_start(offsets[:], offs)
        for q in range(P // QUADRANT):
            nc.sync.dma_start(
                scale_table[QUADRANT * q : QUADRANT * q + PACK * PASSES, :].bitcast(I32),
                x_scales[:, PACK * q : PACK * (q + 1), :].bitcast(I32),
            )

        zero = sb.tile([P, 1], F32, name="zero")
        zero_sum = sb.tile([P, 1], F32, name="zero_sum")
        nc.vector.tensor_tensor(zero_sum[:], zero_a[:], zero_b[:], ALU.add)
        nc.scalar.activation(zero[:], zero_sum[:], ACT.Sqrt)

        word_table1 = sb.tile([P, T], U32, name="word_table1", tag="late", align_bytes=ALIGN)
        weights = sb.tile([P, PACK * (PASSES * H + 2 * N)], F32, name="weights", tag="weights")

        def raw_rows(first, width):
            return weights[:, PACK * first : PACK * (first + width)].rearrange("p (j c) -> p j c", j=PACK)

        w1_raw = [raw_rows(g * H, H) for g in range(PASSES)]
        w2_raw, w3_raw = raw_rows(PASSES * H, N), raw_rows(PASSES * H + N, N)
        for g in range(PASSES):
            load_rows(w1_raw[g], w1[K_PASS * g : K_PASS * (g + 1), :])
        load_words(word_table1, 1)

        identity = sb.tile([P, P], F32, name="identity")
        make_identity(nc, identity[:])

        banks = [ps.tile([P, K_PASS], F32, name="bank%d" % b) for b in range(8)]

        x_code0 = sb.tile([P, S], U32, name="x_code0", align_bytes=ALIGN)
        nc.vector.tensor_copy(x_code0[:], word_table0[:].indirect(offsets[:]))
        x_scale = sb.tile([P, S], U8, name="x_scale", align_bytes=ALIGN)
        nc.vector.tensor_copy(x_scale[:], scale_table[:].indirect(offsets[:]))

        w1_mx = []
        for g in range(PASSES):
            w1_rounded = sb.tile([P, H * PACK], BF16, name="w1_rounded%d" % g, align_bytes=ALIGN)
            split = W1_SCALAR_COLS[g]
            nc.scalar.copy(*four_rows_side_by_side(w1_rounded[:, : PACK * split], w1_raw[g][:, :, :split]))
            nc.vector.tensor_copy(*four_rows_side_by_side(w1_rounded[:, PACK * split :], w1_raw[g][:, :, split:]))
            w1_mx.append(quantize("w1_%d" % g, w1_rounded, H, "w1_code%d" % g))

        load_rows(w2_raw, w2)
        load_rows(w3_raw, w3)

        h_bank = [[banks[7], banks[2]], [banks[2], banks[1]], [banks[0], banks[1]]]
        early = ((C, 0), (C, 1), (B, 0), (A, 0))
        x_code1 = sb.tile([P, S], U32, name="x_code1", align_bytes=ALIGN)
        x_code = (x_code0, x_code1)

        def first_product(g, d, h):
            frames = slice(V * d + P * h, V * d + P * (h + 1))
            nc.tensor.matmul_mx(
                h_bank[d][h][:],
                lhsT=x_code[g][:, frames].bitcast(FP8X4),
                lhsT_scale=x_scale[PACK * g : P, frames],
                rhs=w1_mx[g][0][:].bitcast(FP8X4),
                rhs_scale=w1_mx[g][1][:],
                start=(g == 0),
                stop=(g == PASSES - 1),
            )

        def both_passes(d, h):
            for g in range(PASSES):
                first_product(g, d, h)

        for d, h in early:
            first_product(0, d, h)
        for d in (C, B, A):
            piece = offsets[:, LIST_COLS * d : LIST_COLS * (d + 1)]
            nc.vector.tensor_copy(x_code1[:, V * d : V * (d + 1)], word_table1[:].indirect(piece))
            for h in range(HALVES):
                if (d, h) in early:
                    first_product(1, d, h)

        w23_rounded = sb.tile([P, 2 * N * PACK], BF16, name="w23_rounded", tag="late", align_bytes=ALIGN)
        w3_split = PACK * (N + W3_GPSIMD_COLS)
        for rounded, raw in (
            (w23_rounded[:, : PACK * N], w2_raw),
            (w23_rounded[:, PACK * N : w3_split], w3_raw[:, :, :W3_GPSIMD_COLS]),
        ):
            nc.gpsimd.tensor_scalar(*four_rows_side_by_side(rounded, raw), 1.0, 0.0, ALU.mult, ALU.add)

        def dealt(bank):
            return bank[:].rearrange("p (m t) -> p t m", t=PACK)

        def by_t(tile):
            return tile[:].rearrange("p (t m) -> p t m", t=PACK)

        def term(name):
            return [sb.tile([P, H], F32, name="%s%d" % (name, h), align_bytes=ALIGN) for h in range(HALVES)]

        c_scaled, pair, gap, edge, gap_sq, edge_sq = (term(n) for n in ("c_scaled", "pair", "gap", "edge", "gap_sq", "edge_sq"))
        for h in range(HALVES):
            nc.scalar.activation(by_t(c_scaled[h]), dealt(h_bank[C][h]), ACT.Copy, scale=1.5)
        both_passes(B, 1)
        for h in range(HALVES):
            b_values = dealt(h_bank[B][h])
            nc.vector.scalar_tensor_tensor(by_t(pair[h]), b_values, 1.5, by_t(c_scaled[h]), ALU.mult, ALU.add)
            nc.vector.scalar_tensor_tensor(by_t(gap[h]), b_values, 1.5, by_t(c_scaled[h]), ALU.mult, ALU.subtract)
            if h == 0:
                both_passes(A, 1)
            nc.scalar.activation(gap_sq[h][:], gap[h][:], ACT.Square, bias=zero[:], scale=1.0 / math.sqrt(3.0))
            for lo, hi in ((0, PACK),) if h == 0 else ((0, PACK // 2), (PACK // 2, PACK)):
                nc.vector.scalar_tensor_tensor(
                    by_t(edge[h])[:, lo:hi, :],
                    by_t(pair[h])[:, lo:hi, :],
                    -1.0 / 3.0,
                    dealt(h_bank[A][h])[:, lo:hi, :],
                    ALU.mult,
                    ALU.add,
                )
                nc.scalar.activation(edge_sq[h][:, P * lo : P * hi], edge[h][:, P * lo : P * hi], ACT.Square, bias=zero[:])

        nc.scalar.copy(*four_rows_side_by_side(w23_rounded[:, w3_split:], w3_raw[:, :, W3_GPSIMD_COLS:]))
        w23_code, w23_scale = quantize("w23", w23_rounded, 2 * N, "pair1")

        def turn_and_add(bank, first, second):
            for n, tile in enumerate((first, second)):
                for t in range(PACK):
                    nc.tensor.matmul(
                        bank[:, P * t : P * (t + 1)],
                        tile[:, P * t : P * (t + 1)],
                        identity[:],
                        is_transpose=True,
                        start=(n == 0 and t == 0),
                        stop=(n == 1 and t == PACK - 1),
                    )

        def four_t_side_by_side(rounded, bank):
            return rounded[:].rearrange("p (v t) -> p v t", t=PACK), bank[:].rearrange("p (t v) -> p v t", t=PACK)

        sum_bank = [banks[3], banks[5]]
        square_bank = [banks[4], banks[6]]
        out_bank = [[banks[0], banks[7]], [banks[1], banks[3]]]
        mean_tag = ("mean0", "late")
        dev_tag = ("edge1", "dev1")
        mean_code_tag = ("edge_sq1", "mean_code1")
        dev_code_tag = ("dev_code0", "late")
        for h in range(HALVES):
            turn_and_add(sum_bank[h], pair[h], edge[h])
            turn_and_add(square_bank[h], gap_sq[h], edge_sq[h])

            mean = sb.tile([P, P * PACK], BF16, name="mean%d" % h, tag=mean_tag[h], align_bytes=ALIGN)
            if h == 0:
                nc.scalar.activation(*four_t_side_by_side(mean, sum_bank[h]), ACT.Copy, scale=1.0 / 3.0)
            else:
                nc.vector.tensor_scalar(*four_t_side_by_side(mean, sum_bank[h]), 1.0 / 3.0, None, ALU.mult)
            dev = sb.tile([P, P * PACK], BF16, name="dev%d" % h, tag=dev_tag[h], align_bytes=ALIGN)
            nc.scalar.activation(*four_t_side_by_side(dev, square_bank[h]), ACT.Sqrt, bias=zero[:], scale=2.0 / 9.0)
            stats = (quantize("mean_mx%d" % h, mean, P, mean_code_tag[h]), quantize("dev_mx%d" % h, dev, P, dev_code_tag[h]))

            for u, (code, scale) in enumerate(stats):
                for m in range(N // P):
                    cols = slice(N * u + P * m, N * u + P * (m + 1))
                    nc.tensor.matmul_mx(
                        out_bank[h][m][:, 0:P],
                        lhsT=w23_code[:, cols].bitcast(FP8X4),
                        lhsT_scale=w23_scale[:, cols],
                        rhs=code[:].bitcast(FP8X4),
                        rhs_scale=scale[:],
                        start=(u == 0),
                        stop=(u == 1),
                    )

            for m in range(N // P):
                result = sb.tile([P, P], F32, name="result%d_%d" % (h, m))
                if h == 1 and m == 0:
                    nc.vector.tensor_copy(result[:], out_bank[h][m][:, 0:P])
                else:
                    nc.scalar.copy(result[:], out_bank[h][m][:, 0:P])
                queue = nc.scalar if h == 1 and m == 1 else nc.sync
                queue.dma_start(out[P * m : P * (m + 1), P * h : P * (h + 1)], result[:])
